import numpy as np
import ml_dtypes


def mxq(x, axis, fmt="e4m3"):
    dtype, down = {"e4m3": (ml_dtypes.float8_e4m3fn, 7), "e5m2": (ml_dtypes.float8_e5m2, 14)}[fmt]
    v = np.moveaxis(np.asarray(x, np.float32).astype(ml_dtypes.bfloat16).astype(np.float64), axis, -1)
    blocks = v.reshape(v.shape[:-1] + (-1, 32))
    amax = np.abs(blocks).max(-1, keepdims=True)
    byte = np.maximum(np.where(amax > 0, np.frexp(amax)[1] - 1 + 127, 0) - down, 1)
    scale = np.exp2(byte - 127.0)
    codes = (blocks / scale).astype(np.float32).astype(dtype).astype(np.float64)
    return np.moveaxis((codes * scale).reshape(v.shape), -1, axis)


WIDE = False


def mx_kscale(k):
    if not WIDE:
        return np.ones(k)
    levels = np.array([30, -30])
    if k % 512:
        return np.exp2(np.random.permutation(np.resize(levels, k // 32))).repeat(32)
    a = np.empty((k // 512, 16))
    for p in range(k // 512):
        a[p, :8] = np.random.permutation(np.resize(levels, 8))
        for g in range(8):
            far = levels[np.abs(levels - a[p, g]) >= 10]
            a[p, g + 8] = far[np.random.randint(len(far))]
    return np.exp2(a.ravel()).repeat(32)


BF16 = ml_dtypes.bfloat16


def bf(x):
    return np.asarray(x, np.float32).astype(BF16)


def f64(x):
    return np.asarray(x).astype(np.float64)


M, I, J, D, N = 1024, 16, 128, 1024, 1024


def setup_inputs():
    t, s = mx_kscale(I * J), mx_kscale(D)
    return {
        "a": bf(np.random.standard_normal((M, I))),
        "b": bf(np.random.standard_normal((M, J))),
        "c": bf((1 + 0.1 * np.random.standard_normal((I, J))) * t.reshape(I, J)),
        "core": bf(np.random.standard_normal((I * J, N)) / np.sqrt(I * J) / t[:, None]),
        "x": bf(np.random.standard_normal((M, D)) * s),
        "w": bf(np.random.standard_normal((D, N)) / np.sqrt(D) / s[:, None]),
        "bias": bf(0.3 * np.random.standard_normal(N)),
    }


def reference(a, b, c, core, x, w, bias):
    z = f64(a)[:, :, None] * f64(b)[:, None, :] * f64(c)
    z = z.reshape(M, I * J)
    zq = mxq(z, 1, "e5m2")
    gq = mxq(f64(core), 0, "e4m3")
    xq = mxq(f64(x), 1, "e4m3")
    wq = mxq(f64(w), 0, "e4m3")
    h = (zq @ gq) + (xq @ wq)
    return np.tanh(h + f64(bias))

@@ -1,0 +1,323 @@
+from contextlib import ExitStack
+
+import concourse.mybir as mybir
+from concourse.masks import make_identity
+
+M, I, J, D, N = 1024, 16, 128, 1024, 1024
+FLOPS = 2 * M * N * (I * J + D)
+
+F32 = mybir.dt.float32
+BF16 = mybir.dt.bfloat16
+U32 = mybir.dt.uint32
+U8 = mybir.dt.uint8
+E4M3 = mybir.dt.float8_e4m3fn_x4
+E5M2 = mybir.dt.float8_e5m2_x4
+MULT = mybir.AluOpType.mult
+ADD = mybir.AluOpType.add
+TANH = mybir.ActivationFunctionType.Tanh
+
+P = 128
+PACK = 4
+K_PASS = P * PACK
+N_TILE = 512
+M_TILES = M // P
+N_HALVES = N // N_TILE
+Z_PASSES = I * J // K_PASS
+X_PASSES = D // K_PASS
+PASSES = Z_PASSES + X_PASSES
+PIECES = PASSES * N_HALVES
+ACC_BANKS = 4
+TURN_BANKS = 3
+MX_LATE = 4
+HEAD = []
+ROUND_PIECES = [["scalar","gpsimd"],["scalar","gpsimd"],["scalar","gpsimd"],["scalar","gpsimd"],["scalar","gpsimd"],["scalar"]]
+G_COLS = 448
+MX_BEFORE = 6
+MX_AFTER = 4
+X_AFTER = [0,3,5,7,9,11,11,11]
+
+
+def tile_tensor_product_core_s2_kernel(tc, a, b, c, core, x, w, bias, out):
+    nc = tc.nc
+    with ExitStack() as ctx:
+        keep = ctx.enter_context(tc.tile_pool(name="keep", bufs=1))
+        work = ctx.enter_context(tc.tile_pool(name="work", bufs=2))
+        psum = ctx.enter_context(tc.psum_pool(name="psum", bufs=1))
+        ctx.enter_context(tc.manual_schedule())
+
+        x_rows = x.rearrange("(p t) d -> p t d", t=M_TILES)
+        out_rows = out.rearrange("(p t) n -> p t n", t=M_TILES)
+
+        b_sb = keep.tile([P, M_TILES * J], BF16, name="b_sb")
+        c_sb = keep.tile([P, I * J // P], BF16, name="c_sb")
+        a_sb = keep.tile([P, M_TILES * I], BF16, name="a_sb")
+        bias_sb = keep.tile([P, N // P], BF16, name="bias_sb")
+        nc.sync.dma_start(out=b_sb[:], in_=b.rearrange("(p t) j -> p (t j)", t=M_TILES))
+        nc.sync.dma_start(out=c_sb[:], in_=c.rearrange("i (r s) -> (i r) s", s=I * J // P))
+        nc.sync.dma_start(out=a_sb[:], in_=a.rearrange("(p t) i -> p (t i)", t=M_TILES))
+        raw = []
+        x_sb = {}
+
+        def load_x(mt):
+            x_sb[mt] = keep.tile([P, D], BF16, name="x_sb%d" % mt)
+            nc.sync.dma_start(out=x_sb[mt][:], in_=x_rows[:, mt, :])
+
+        for piece in range(PIECES):
+            half, g = divmod(piece, PASSES)
+            cols = slice(half * N_TILE, (half + 1) * N_TILE)
+            if g < Z_PASSES:
+                rows = core[g * K_PASS:(g + 1) * K_PASS, cols]
+            else:
+                rows = w[(g - Z_PASSES) * K_PASS:(g - Z_PASSES + 1) * K_PASS, cols]
+            tile = keep.tile([P, PACK, N_TILE], BF16, name="raw%d" % piece)
+            nc.sync.dma_start(out=tile[:], in_=rows.rearrange("(p t) n -> p t n", t=PACK))
+            raw.append(tile)
+            if piece == 0:
+                nc.sync.dma_start(out=bias_sb[:], in_=bias.rearrange("(p s) -> p s", p=P))
+            for mt in range(M_TILES):
+                if X_AFTER[mt] == piece:
+                    load_x(mt)
+
+        ident = keep.tile([P, P], F32, name="ident")
+        make_identity(nc, ident[:])
+        warm = keep.tile([P, 1], F32, name="warm")
+        nc.scalar.activation(out=warm[:], in_=ident[:, 0:1], func=TANH)
+
+        b_words = b_sb[:].bitcast(F32)
+        bt_ps = psum.tile([P, 4, P], F32, name="bt_ps", tag="acc0")
+        for h in range(2):
+            for u in range(2):
+                nc.tensor.transpose(bt_ps[:, 2 * h + u, :], b_words[:, 256 * h + u:256 * (h + 1):2], ident[:])
+        bt_sb = keep.tile([P, 4, P], F32, name="bt_sb")
+        nc.scalar.copy(out=bt_sb[:], in_=bt_ps[:])
+
+        c_words = c_sb[:].bitcast(F32)
+        c_all = keep.tile([P, I, 2, 32], F32, name="c_all")
+        for u in range(2):
+            c_ps = psum.tile([P, 4, P], F32, name="c_ps", tag="acc%d" % (1 + u))
+            for s in range(4):
+                word = 2 * s + u
+                nc.tensor.transpose(c_ps[:, s, :], c_words[:, word:word + 1].to_broadcast([P, P]), ident[:])
+            nc.scalar.copy(
+                out=c_all[:, :, u, :].rearrange("p i (r s) -> p i r s", s=4),
+                in_=c_ps[:].rearrange("p s (i r) -> p i r s", r=8),
+            )
+        b_ps = psum.tile([P, 4, P], F32, name="b_ps", tag="b_ps")
+        for hu in range(4):
+            nc.tensor.transpose(b_ps[:, hu, :], bt_sb[:, hu, :], ident[:])
+        b_pairs = b_ps[:].rearrange("p a m -> p (a m)").bitcast(BF16).rearrange("p (h u t e) -> p h u t e", h=2, u=2, t=4)
+        c_pairs = c_all[:].rearrange("p i u q -> p (i u q)").bitcast(BF16).rearrange("p (i u e) -> p i u e", i=I, u=2)
+
+        bias_all = keep.tile([P, P, 4], F32, name="bias_all")
+        bias_row = bias_all[:].rearrange("p q s -> p (q s)").bitcast(BF16)
+
+        z_sb = {}
+        grouped = {}
+        zt = {}
+        xt = {}
+        lhs = {}
+        rhs = {}
+
+        def multiply_z(mt, half):
+            z = work.tile([P, 2, 2, 4, 64], BF16, name="z", bufs=3)
+            z_sb[mt, half] = z
+            for g in range(2):
+                for il in range(4):
+                    i = 8 * half + 4 * g + il
+                    nc.vector.scalar_tensor_tensor(
+                        out=z[:, g, :, il, :],
+                        in0=b_pairs[:, mt // 4, :, mt % 4, :],
+                        scalar=a_sb[:, mt * I + i:mt * I + i + 1],
+                        in1=c_pairs[:, i, :, :],
+                        op0=MULT,
+                        op1=MULT,
+                    )
+
+        def turn(words, dst):
+            bank = psum.tile([P, 2, 2, P], F32, name="bank", tag="turn", bufs=TURN_BANKS)
+            for g in range(2):
+                for u in range(2):
+                    nc.tensor.transpose(bank[:, g, u, :], words(g, u), ident[:])
+            return lambda: nc.scalar.copy(out=dst, in_=bank[:].rearrange("p g u m -> p g m u"))
+
+        def turn_tile(mt):
+            xw = x_sb[mt][:].bitcast(F32)
+            xt[mt] = work.tile([P, X_PASSES, P, 2], F32, name="xt", align_bytes=64, tag="stage%d" % ((mt + 1) % 2), bufs=1)
+            zt[mt] = work.tile([P, Z_PASSES, P, 2], F32, name="zt", align_bytes=64)
+            for part in ("z0", "z1", "x"):
+                if part == "x":
+                    turn(lambda g, u: xw[:, 256 * g + u:256 * (g + 1):2], xt[mt][:])()
+                else:
+                    half = 0 if part == "z0" else 1
+                    zw = z_sb[mt, half][:].rearrange("p g u i e -> p (g u i e)").bitcast(F32)
+                    turn(lambda g, u: zw[:, P * (2 * g + u):P * (2 * g + u + 1)], zt[mt][:, 2 * half:2 * half + 2, :, :])()
+
+        def quantize(src, width, fmt, name):
+            codes = keep.tile([P, width], U32, name=name + "_codes", align_bytes=64)
+            scales = keep.tile([P, width], U8, name=name + "_scales", align_bytes=64)
+            nc.vector.quantize_mx(out=codes[:].bitcast(fmt), scales=scales[:], in_=src)
+            return codes, scales
+
+        def quantize_tile(mt):
+            for src, first, passes, fmt, name in ((zt[mt], 0, Z_PASSES, E5M2, "z%d" % mt), (xt[mt], Z_PASSES, X_PASSES, E4M3, "x%d" % mt)):
+                codes, scales = quantize(src[:].rearrange("p g m u -> p (g m u)").bitcast(BF16), passes * P, fmt, name)
+                for g in range(passes):
+                    lhs[mt, first + g] = (codes[:, g * P:(g + 1) * P].bitcast(fmt), scales[:, g * P:(g + 1) * P])
+
+        def interleave(piece, engine, lo=0, hi=N_TILE, tag=None):
+            tag = tag or engine
+            if piece not in grouped:
+                grouped[piece] = work.tile([P, N_TILE, PACK], BF16, name="grouped", tag=tag, align_bytes=64, bufs=1 if tag.startswith("stage") else 2)
+            cols = slice(lo, hi)
+            if engine == "gpsimd":
+                nc.gpsimd.tensor_scalar(out=grouped[piece][:, cols, :], in0=raw[piece][:, :, cols].rearrange("p t n -> p n t"),
+                                        scalar1=1.0, scalar2=0.0, op0=MULT, op1=ADD)
+                return
+            dst = grouped[piece][:, cols, :].rearrange("p (q e) t -> p q t e", e=4)
+            src = raw[piece][:, :, cols].rearrange("p t (q e) -> p q t e", e=4)
+            if engine == "scalar":
+                nc.scalar.copy(out=dst, in_=src)
+            else:
+                nc.vector.tensor_copy(out=dst, in_=src)
+
+        def quantize_piece(piece):
+            codes, scales = quantize(grouped[piece][:].rearrange("p n t -> p (n t)"), N_TILE, E4M3, "w%d" % piece)
+            rhs[divmod(piece, PASSES)] = (codes[:].bitcast(E4M3), scales[:])
+
+        waiting = [(mt, half) for half in range(N_HALVES) for mt in range(M_TILES)]
+        free_banks = list(range(ACC_BANKS))
+        opened = []
+        state = {}
+        closed = []
+        drain_next = []
+
+        issued = [0]
+        closed_at = {}
+
+        def multiply(budget):
+            for tile in opened + waiting:
+                mt, half = tile
+                ready = [g for g in range(PASSES) if (mt, g) in lhs and (half, g) in rhs]
+                if tile not in state:
+                    partial = [t for t in opened if any((t[1], g) not in rhs for g in range(PASSES))]
+                    early = half > 0 and any((half, g) not in rhs for g in range(PASSES)) and len(partial) >= 2
+                    if not ready or budget == 0 or not free_banks or early:
+                        continue
+                    bank = free_banks[0]
+                    free_banks.remove(bank)
+                    acc = psum.tile([P, N_TILE], F32, name="acc", tag="acc%d" % bank)
+                    state[tile] = (acc, bank, [])
+                    waiting.remove(tile)
+                    opened.append(tile)
+                acc, bank, done = state[tile]
+                for g in ready:
+                    if g in done or budget == 0:
+                        continue
+                    done.append(g)
+                    budget = budget - 1
+                    issued[0] = issued[0] + 1
+                    nc.tensor.matmul_mx(
+                        out=acc[:], lhsT=lhs[mt, g][0], lhsT_scale=lhs[mt, g][1], rhs=rhs[half, g][0], rhs_scale=rhs[half, g][1],
+                        start=len(done) == 1, stop=len(done) == PASSES,
+                    )
+                if len(done) == PASSES:
+                    closed.append(tile)
+                    closed_at[tile] = issued[0]
+                    opened.remove(tile)
+            return budget
+
+        def drain(lag):
+            tails = []
+            for mt, half in [t for t in closed if issued[0] - closed_at[t] >= lag]:
+                acc, bank, done = state[mt, half]
+                cols = slice(half * N_TILE, (half + 1) * N_TILE)
+                pre = work.tile([P, N_TILE], F32, name="pre", bufs=6)
+                nc.vector.tensor_tensor(out=pre[:], in0=acc[:], in1=bias_row[:, cols], op=ADD)
+                free_banks.append(bank)
+                closed.remove((mt, half))
+                tails.append((mt, cols, pre))
+            return tails
+
+        def tick(n):
+            issued[0] = issued[0] + n
+
+        def warm_up(n):
+            codes, scales = rhs[0, 0]
+            for k in range(n):
+                spare = psum.tile([P, N_TILE], F32, name="spare", tag="acc%d" % (ACC_BANKS - 1))
+                nc.tensor.matmul_mx(out=spare[:], lhsT=codes[:, 0:P], lhsT_scale=scales[:, 0:P], rhs=codes, rhs_scale=scales, start=True, stop=True)
+
+        def finish(tails):
+            for mt, cols, pre in tails:
+                y = work.tile([P, N_TILE], F32, name="y", bufs=4)
+                nc.scalar.activation(out=y[:], in_=pre[:], func=TANH)
+                nc.sync.dma_start(out=out_rows[:, mt, cols], in_=y[:])
+
+        def spread_bias():
+            bias_words = bias_sb[:].bitcast(F32)
+            bias_ps = psum.tile([P, 4, P], F32, name="bias_ps", tag="acc3")
+            for s in range(4):
+                nc.tensor.transpose(bias_ps[:, s, :], bias_words[:, s:s + 1].to_broadcast([P, P]), ident[:])
+            nc.scalar.copy(out=bias_all[:], in_=bias_ps[:].rearrange("p s q -> p q s"))
+
+        def pieces_of(rnd, engine):
+            first = 1 + sum(len(r) for r in ROUND_PIECES[:rnd])
+            if rnd >= len(ROUND_PIECES):
+                return []
+            return [first + n for n, e in enumerate(ROUND_PIECES[rnd]) if e == engine]
+
+        interleave(0, "vector", tag="stage0")
+        quantize_piece(0)
+        warm_up(0)
+        multiply_z(0, 0)
+        for p in pieces_of(0, "scalar")[:1]:
+            interleave(p, "scalar", 0, 256)
+        for mt in range(M_TILES):
+            for p in pieces_of(mt, "gpsimd"):
+                interleave(p, "gpsimd", 0, G_COLS, tag="stage%d" % (mt % 2))
+            for p in pieces_of(mt, "scalar")[:1]:
+                interleave(p, "scalar", 256, N_TILE)
+            if G_COLS < N_TILE:
+                for p in pieces_of(mt, "gpsimd"):
+                    interleave(p, "scalar", G_COLS, N_TILE)
+            multiply_z(mt, 1)
+            turn_tile(mt)
+            if mt == 0:
+                spread_bias()
+            if mt + 1 < M_TILES:
+                multiply_z(mt + 1, 0)
+            if mt <= -1:
+                warm_up(0)
+            tails = drain(0)
+            left = multiply(11)
+            finish(tails)
+            for p in pieces_of(mt, "scalar")[1:]:
+                interleave(p, "scalar")
+            for p in pieces_of(mt + 1, "scalar")[:1]:
+                interleave(p, "scalar", 0, 256)
+            pass
+            for p in pieces_of(mt, "vector"):
+                interleave(p, "vector")
+            for p in pieces_of(mt, "scalar") + pieces_of(mt, "gpsimd") + pieces_of(mt, "vector"):
+                quantize_piece(p)
+                left = multiply(left)
+            quantize_tile(mt)
+            left = multiply(left)
+            if mt <= -1:
+                warm_up(min(left, 0))
+        while waiting or opened or len(closed) > 1:
+            multiply(PASSES)
+            if waiting or opened:
+                finish(drain(1))
+            else:
+                finish(drain(1))
+        mt, half = closed[0]
+        acc = state[mt, half][0]
+        tails = []
+        for part in range(2):
+            cols = slice(half * N_TILE + part * 256, half * N_TILE + (part + 1) * 256)
+            pre = work.tile([P, 256], F32, name="pre_last")
+            nc.vector.tensor_tensor(out=pre[:], in0=acc[:, part * 256:(part + 1) * 256], in1=bias_row[:, cols], op=ADD)
+            y = work.tile([P, 256], F32, name="y_last")
+            nc.scalar.activation(out=y[:], in_=pre[:], func=TANH)
+            nc.sync.dma_start(out=out_rows[:, mt, cols], in_=y[:])

@@ -20,21 +20,26 @@ P = 128
 PACK = 4
 K_PASS = P * PACK
 N_TILE = 512
-M_TILES = M // P
-N_HALVES = N // N_TILE
+ROW_TILES = M // P
+HALVES = N // N_TILE
 Z_PASSES = I * J // K_PASS
 X_PASSES = D // K_PASS
 PASSES = Z_PASSES + X_PASSES
-PIECES = PASSES * N_HALVES
+I_PER_PASS = K_PASS // J
+J_PAIRS = J // PACK
+B_GROUP = P // J_PAIRS
+PIECES = HALVES * PASSES
 ACC_BANKS = 4
 TURN_BANKS = 3
-MX_LATE = 4
-HEAD = []
-ROUND_PIECES = [["scalar","gpsimd"],["scalar","gpsimd"],["scalar","gpsimd"],["scalar","gpsimd"],["scalar","gpsimd"],["scalar"]]
-G_COLS = 448
-MX_BEFORE = 6
-MX_AFTER = 4
-X_AFTER = [0,3,5,7,9,11,11,11]
+GPSIMD_COLS = 416
+ROUND_PASSES = 13
+MAX_EARLY = 3
+
+
+def round_pieces(row):
+    if row == 0:
+        return [1, 2, 3]
+    return [p for p in (2 * row + 2, 2 * row + 3) if p < PIECES]
 
 
 def tile_tensor_product_core_s2_kernel(tc, a, b, c, core, x, w, bias, out):
@@ -45,164 +50,191 @@ def tile_tensor_product_core_s2_kernel(tc, a, b, c, core, x, w, bias, out):
         psum = ctx.enter_context(tc.psum_pool(name="psum", bufs=1))
         ctx.enter_context(tc.manual_schedule())
 
-        x_rows = x.rearrange("(p t) d -> p t d", t=M_TILES)
-        out_rows = out.rearrange("(p t) n -> p t n", t=M_TILES)
+        b_rows = b.rearrange("(p r) j -> p (r j)", r=ROW_TILES)
+        x_rows = x.rearrange("(p r) d -> p r d", r=ROW_TILES)
+        out_rows = out.rearrange("(p r) n -> p r n", r=ROW_TILES)
 
-        b_sb = keep.tile([P, M_TILES * J], BF16, name="b_sb")
-        c_sb = keep.tile([P, I * J // P], BF16, name="c_sb")
-        a_sb = keep.tile([P, M_TILES * I], BF16, name="a_sb")
-        bias_sb = keep.tile([P, N // P], BF16, name="bias_sb")
-        nc.sync.dma_start(out=b_sb[:], in_=b.rearrange("(p t) j -> p (t j)", t=M_TILES))
-        nc.sync.dma_start(out=c_sb[:], in_=c.rearrange("i (r s) -> (i r) s", s=I * J // P))
-        nc.sync.dma_start(out=a_sb[:], in_=a.rearrange("(p t) i -> p (t i)", t=M_TILES))
-        raw = []
-        x_sb = {}
+        b_sb, x_sb, raw = [], [], []
 
-        def load_x(mt):
-            x_sb[mt] = keep.tile([P, D], BF16, name="x_sb%d" % mt)
-            nc.sync.dma_start(out=x_sb[mt][:], in_=x_rows[:, mt, :])
+        def load_b(group):
+            tile = keep.tile([P, B_GROUP * J], BF16, name="b_sb%d" % group)
+            nc.sync.dma_start(out=tile[:], in_=b_rows[:, group * B_GROUP * J:(group + 1) * B_GROUP * J])
+            b_sb.append(tile)
 
-        for piece in range(PIECES):
+        def load_x(row):
+            tile = keep.tile([P, D], BF16, name="x_sb%d" % row)
+            nc.sync.dma_start(out=tile[:], in_=x_rows[:, row, :])
+            x_sb.append(tile)
+
+        def load_piece(piece):
             half, g = divmod(piece, PASSES)
-            cols = slice(half * N_TILE, (half + 1) * N_TILE)
-            if g < Z_PASSES:
-                rows = core[g * K_PASS:(g + 1) * K_PASS, cols]
-            else:
-                rows = w[(g - Z_PASSES) * K_PASS:(g - Z_PASSES + 1) * K_PASS, cols]
+            source, first = (core, g * K_PASS) if g < Z_PASSES else (w, (g - Z_PASSES) * K_PASS)
+            rows = source[first:first + K_PASS, half * N_TILE:(half + 1) * N_TILE]
             tile = keep.tile([P, PACK, N_TILE], BF16, name="raw%d" % piece)
             nc.sync.dma_start(out=tile[:], in_=rows.rearrange("(p t) n -> p t n", t=PACK))
             raw.append(tile)
-            if piece == 0:
+
+        c_sb = keep.tile([P, I * J // P], BF16, name="c_sb")
+        a_sb = keep.tile([P, ROW_TILES * I], BF16, name="a_sb")
+        bias_sb = keep.tile([P, N // P], BF16, name="bias_sb")
+        load_b(0)
+        nc.sync.dma_start(out=c_sb[:], in_=c.rearrange("i (r s) -> (i r) s", s=I * J // P))
+        load_piece(0)
+        nc.sync.dma_start(out=a_sb[:], in_=a.rearrange("(p r) i -> p (r i)", r=ROW_TILES))
+        for row in range(ROW_TILES):
+            for piece in round_pieces(row):
+                load_piece(piece)
+            load_x(row)
+            if row == 0:
+                load_b(1)
                 nc.sync.dma_start(out=bias_sb[:], in_=bias.rearrange("(p s) -> p s", p=P))
-            for mt in range(M_TILES):
-                if X_AFTER[mt] == piece:
-                    load_x(mt)
 
         ident = keep.tile([P, P], F32, name="ident")
         make_identity(nc, ident[:])
-        warm = keep.tile([P, 1], F32, name="warm")
-        nc.scalar.activation(out=warm[:], in_=ident[:, 0:1], func=TANH)
+        table_warm = keep.tile([P, 1], F32, name="table_warm")
+        nc.scalar.activation(out=table_warm[:], in_=ident[:, 0:1], func=TANH)
 
-        b_words = b_sb[:].bitcast(F32)
-        bt_ps = psum.tile([P, 4, P], F32, name="bt_ps", tag="acc0")
-        for h in range(2):
+        b_ps = psum.tile([P, ROW_TILES // B_GROUP, 2, P], F32, name="b_ps")
+        b_turned = {}
+
+        def turn_b_out(group):
+            pairs = b_sb[group][:].bitcast(F32)
+            ps = psum.tile([P, 2, P], F32, name="b_turn", tag="turn", bufs=TURN_BANKS)
             for u in range(2):
-                nc.tensor.transpose(bt_ps[:, 2 * h + u, :], b_words[:, 256 * h + u:256 * (h + 1):2], ident[:])
-        bt_sb = keep.tile([P, 4, P], F32, name="bt_sb")
-        nc.scalar.copy(out=bt_sb[:], in_=bt_ps[:])
+                nc.tensor.transpose(ps[:, u, :], pairs[:, u::2], ident[:])
+            b_turned[group] = work.tile([P, 2, P], F32, name="b_turned")
+            nc.scalar.copy(out=b_turned[group][:], in_=ps[:])
 
+        def turn_b_back(group):
+            for u in range(2):
+                nc.tensor.transpose(b_ps[:, group, u, :], b_turned[group][:, u, :], ident[:])
+
+        turn_b_out(0)
         c_words = c_sb[:].bitcast(F32)
-        c_all = keep.tile([P, I, 2, 32], F32, name="c_all")
+        c_all = keep.tile([P, I, 2, J_PAIRS], F32, name="c_all")
         for u in range(2):
-            c_ps = psum.tile([P, 4, P], F32, name="c_ps", tag="acc%d" % (1 + u))
+            ps = psum.tile([P, 4, P], F32, name="c_spread", tag="turn", bufs=TURN_BANKS)
             for s in range(4):
                 word = 2 * s + u
-                nc.tensor.transpose(c_ps[:, s, :], c_words[:, word:word + 1].to_broadcast([P, P]), ident[:])
+                nc.tensor.transpose(ps[:, s, :], c_words[:, word:word + 1].to_broadcast([P, P]), ident[:])
             nc.scalar.copy(
                 out=c_all[:, :, u, :].rearrange("p i (r s) -> p i r s", s=4),
-                in_=c_ps[:].rearrange("p s (i r) -> p i r s", r=8),
+                in_=ps[:].rearrange("p s (i r) -> p i r s", i=I),
             )
-        b_ps = psum.tile([P, 4, P], F32, name="b_ps", tag="b_ps")
-        for hu in range(4):
-            nc.tensor.transpose(b_ps[:, hu, :], bt_sb[:, hu, :], ident[:])
-        b_pairs = b_ps[:].rearrange("p a m -> p (a m)").bitcast(BF16).rearrange("p (h u t e) -> p h u t e", h=2, u=2, t=4)
-        c_pairs = c_all[:].rearrange("p i u q -> p (i u q)").bitcast(BF16).rearrange("p (i u e) -> p i u e", i=I, u=2)
+        turn_b_back(0)
+        b_values = b_ps[:].rearrange("p h u q -> p (h u q)").bitcast(BF16)
+        b_values = b_values.rearrange("p (h u r e) -> p h u r e", u=2, r=B_GROUP, e=2 * J_PAIRS)
+        c_values = c_all[:].rearrange("p i u q -> p (i u q)").bitcast(BF16)
+        c_values = c_values.rearrange("p (i u e) -> p i u e", i=I, u=2)
 
         bias_all = keep.tile([P, P, 4], F32, name="bias_all")
-        bias_row = bias_all[:].rearrange("p q s -> p (q s)").bitcast(BF16)
+        bias_values = bias_all[:].rearrange("p q s -> p (q s)").bitcast(BF16)
 
-        z_sb = {}
-        grouped = {}
-        zt = {}
-        xt = {}
-        lhs = {}
-        rhs = {}
+        def spread_bias():
+            words = bias_sb[:].bitcast(F32)
+            ps = psum.tile([P, 4, P], F32, name="bias_spread", tag="turn", bufs=TURN_BANKS)
+            for s in range(4):
+                nc.tensor.transpose(ps[:, s, :], words[:, s:s + 1].to_broadcast([P, P]), ident[:])
+            nc.scalar.copy(out=bias_all[:], in_=ps[:].rearrange("p s q -> p q s"))
 
-        def multiply_z(mt, half):
-            z = work.tile([P, 2, 2, 4, 64], BF16, name="z", bufs=3)
-            z_sb[mt, half] = z
+        z_sb, z_turned, x_turned, grouped, stationary, moving = {}, {}, {}, {}, {}, {}
+
+        def form_z(row, part):
+            z = work.tile([P, 2, 2, I_PER_PASS, 2 * J_PAIRS], BF16, name="z", bufs=3)
+            z_sb[row, part] = z
             for g in range(2):
-                for il in range(4):
-                    i = 8 * half + 4 * g + il
+                for il in range(I_PER_PASS):
+                    i = (2 * part + g) * I_PER_PASS + il
                     nc.vector.scalar_tensor_tensor(
                         out=z[:, g, :, il, :],
-                        in0=b_pairs[:, mt // 4, :, mt % 4, :],
-                        scalar=a_sb[:, mt * I + i:mt * I + i + 1],
-                        in1=c_pairs[:, i, :, :],
+                        in0=b_values[:, row // B_GROUP, :, row % B_GROUP, :],
+                        scalar=a_sb[:, row * I + i:row * I + i + 1],
+                        in1=c_values[:, i, :, :],
                         op0=MULT,
                         op1=MULT,
                     )
 
-        def turn(words, dst):
-            bank = psum.tile([P, 2, 2, P], F32, name="bank", tag="turn", bufs=TURN_BANKS)
-            for g in range(2):
-                for u in range(2):
-                    nc.tensor.transpose(bank[:, g, u, :], words(g, u), ident[:])
-            return lambda: nc.scalar.copy(out=dst, in_=bank[:].rearrange("p g u m -> p g m u"))
+        def turn(sources, dst):
+            ps = psum.tile([P, 2, 2, P], F32, name="turn", tag="turn", bufs=TURN_BANKS)
+            for n, source in enumerate(sources):
+                nc.tensor.transpose(ps[:, n // 2, n % 2, :], source, ident[:])
+            nc.scalar.copy(out=dst, in_=ps[:].rearrange("p g u m -> p g m u"))
 
-        def turn_tile(mt):
-            xw = x_sb[mt][:].bitcast(F32)
-            xt[mt] = work.tile([P, X_PASSES, P, 2], F32, name="xt", align_bytes=64, tag="stage%d" % ((mt + 1) % 2), bufs=1)
-            zt[mt] = work.tile([P, Z_PASSES, P, 2], F32, name="zt", align_bytes=64)
-            for part in ("z0", "z1", "x"):
-                if part == "x":
-                    turn(lambda g, u: xw[:, 256 * g + u:256 * (g + 1):2], xt[mt][:])()
-                else:
-                    half = 0 if part == "z0" else 1
-                    zw = z_sb[mt, half][:].rearrange("p g u i e -> p (g u i e)").bitcast(F32)
-                    turn(lambda g, u: zw[:, P * (2 * g + u):P * (2 * g + u + 1)], zt[mt][:, 2 * half:2 * half + 2, :, :])()
+        def turn_row_tile(row):
+            z_turned[row] = work.tile([P, Z_PASSES, P, 2], F32, name="z_turned", align_bytes=64)
+            for part in range(2):
+                pairs = z_sb[row, part][:].rearrange("p g u i e -> p (g u i e)").bitcast(F32)
+                turn([pairs[:, P * n:P * (n + 1)] for n in range(4)], z_turned[row][:, 2 * part:2 * part + 2, :, :])
+            x_turned[row] = work.tile([P, X_PASSES, P, 2], F32, name="x_turned", tag=("shared%d" % (row % 2)) if row else "x0", bufs=1, align_bytes=64)
+            pairs = x_sb[row][:].bitcast(F32)
+            turn([pairs[:, 2 * P * g + u:2 * P * (g + 1):2] for g in range(2) for u in range(2)], x_turned[row][:])
 
-        def quantize(src, width, fmt, name):
+        def quantize(values, width, fmt, name):
             codes = keep.tile([P, width], U32, name=name + "_codes", align_bytes=64)
             scales = keep.tile([P, width], U8, name=name + "_scales", align_bytes=64)
-            nc.vector.quantize_mx(out=codes[:].bitcast(fmt), scales=scales[:], in_=src)
+            nc.vector.quantize_mx(out=codes[:].bitcast(fmt), scales=scales[:], in_=values)
             return codes, scales
 
-        def quantize_tile(mt):
-            for src, first, passes, fmt, name in ((zt[mt], 0, Z_PASSES, E5M2, "z%d" % mt), (xt[mt], Z_PASSES, X_PASSES, E4M3, "x%d" % mt)):
-                codes, scales = quantize(src[:].rearrange("p g m u -> p (g m u)").bitcast(BF16), passes * P, fmt, name)
+        def quantize_row_tile(row):
+            for turned, first, passes, fmt, name in (
+                (z_turned[row], 0, Z_PASSES, E5M2, "z%d" % row),
+                (x_turned[row], Z_PASSES, X_PASSES, E4M3, "x%d" % row),
+            ):
+                values = turned[:].rearrange("p g m u -> p (g m u)").bitcast(BF16)
+                codes, scales = quantize(values, passes * P, fmt, name)
                 for g in range(passes):
-                    lhs[mt, first + g] = (codes[:, g * P:(g + 1) * P].bitcast(fmt), scales[:, g * P:(g + 1) * P])
+                    cols = slice(g * P, (g + 1) * P)
+                    stationary[row, first + g] = (codes[:, cols].bitcast(fmt), scales[:, cols])
 
-        def interleave(piece, engine, lo=0, hi=N_TILE, tag=None):
-            tag = tag or engine
-            if piece not in grouped:
-                grouped[piece] = work.tile([P, N_TILE, PACK], BF16, name="grouped", tag=tag, align_bytes=64, bufs=1 if tag.startswith("stage") else 2)
-            cols = slice(lo, hi)
-            if engine == "gpsimd":
-                nc.gpsimd.tensor_scalar(out=grouped[piece][:, cols, :], in0=raw[piece][:, :, cols].rearrange("p t n -> p n t"),
-                                        scalar1=1.0, scalar2=0.0, op0=MULT, op1=ADD)
-                return
-            dst = grouped[piece][:, cols, :].rearrange("p (q e) t -> p q t e", e=4)
-            src = raw[piece][:, :, cols].rearrange("p t (q e) -> p q t e", e=4)
-            if engine == "scalar":
-                nc.scalar.copy(out=dst, in_=src)
-            else:
-                nc.vector.tensor_copy(out=dst, in_=src)
+        def new_grouped(piece, tag, bufs):
+            grouped[piece] = work.tile([P, N_TILE, PACK], BF16, name="grouped", tag=tag, bufs=bufs, align_bytes=64)
+
+        def group_columns(piece, copy, lo, hi):
+            copy(
+                out=grouped[piece][:, lo:hi, :].rearrange("p (q e) t -> p q t e", e=4),
+                in_=raw[piece][:, :, lo:hi].rearrange("p t (q e) -> p q t e", e=4),
+            )
+
+        def group_on_gpsimd(piece, tag, cols):
+            new_grouped(piece, tag, 1)
+            nc.gpsimd.tensor_scalar(
+                out=grouped[piece][:, 0:cols, :],
+                in0=raw[piece][:, :, 0:cols].rearrange("p t n -> p n t"),
+                scalar1=1.0,
+                scalar2=0.0,
+                op0=MULT,
+                op1=ADD,
+            )
+            if cols < N_TILE:
+                group_columns(piece, nc.scalar.copy, cols, N_TILE)
+
+        def group_on_scalar(piece):
+            new_grouped(piece, "scalar_piece", 2)
+            group_columns(piece, nc.scalar.copy, 0, N_TILE)
 
         def quantize_piece(piece):
-            codes, scales = quantize(grouped[piece][:].rearrange("p n t -> p (n t)"), N_TILE, E4M3, "w%d" % piece)
-            rhs[divmod(piece, PASSES)] = (codes[:].bitcast(E4M3), scales[:])
+            values = grouped[piece][:].rearrange("p n t -> p (n t)")
+            codes, scales = quantize(values, N_TILE, E4M3, "w%d" % piece)
+            moving[divmod(piece, PASSES)] = (codes[:].bitcast(E4M3), scales[:])
 
-        waiting = [(mt, half) for half in range(N_HALVES) for mt in range(M_TILES)]
+        waiting = [(row, half) for half in range(HALVES) for row in range(ROW_TILES)]
+        opened, closed = [], []
         free_banks = list(range(ACC_BANKS))
-        opened = []
         state = {}
-        closed = []
-        drain_next = []
 
-        issued = [0]
-        closed_at = {}
+        def lacks_pieces(tile):
+            return any((tile[1], g) not in moving for g in range(PASSES))
 
-        def multiply(budget):
+        def multiply(budget, reserve):
             for tile in opened + waiting:
-                mt, half = tile
-                ready = [g for g in range(PASSES) if (mt, g) in lhs and (half, g) in rhs]
+                row, half = tile
+                ready = [g for g in range(PASSES) if (row, g) in stationary and (half, g) in moving]
                 if tile not in state:
-                    partial = [t for t in opened if any((t[1], g) not in rhs for g in range(PASSES))]
-                    early = half > 0 and any((half, g) not in rhs for g in range(PASSES)) and len(partial) >= 2
-                    if not ready or budget == 0 or not free_banks or early:
+                    if not ready or budget == 0 or not free_banks:
                         continue
+                    if half > 0 and lacks_pieces(tile):
+                        if len([t for t in opened if lacks_pieces(t)]) >= MAX_EARLY or len(free_banks) <= reserve:
+                            continue
                     bank = free_banks[0]
                     free_banks.remove(bank)
                     acc = psum.tile([P, N_TILE], F32, name="acc", tag="acc%d" % bank)
@@ -210,114 +242,99 @@ def tile_tensor_product_core_s2_kernel(tc, a, b, c, core, x, w, bias, out):
                     waiting.remove(tile)
                     opened.append(tile)
                 acc, bank, done = state[tile]
-                for g in ready:
-                    if g in done or budget == 0:
-                        continue
+                for g in [g for g in ready if g not in done][:budget]:
                     done.append(g)
                     budget = budget - 1
-                    issued[0] = issued[0] + 1
                     nc.tensor.matmul_mx(
-                        out=acc[:], lhsT=lhs[mt, g][0], lhsT_scale=lhs[mt, g][1], rhs=rhs[half, g][0], rhs_scale=rhs[half, g][1],
-                        start=len(done) == 1, stop=len(done) == PASSES,
+                        out=acc[:],
+                        lhsT=stationary[row, g][0],
+                        lhsT_scale=stationary[row, g][1],
+                        rhs=moving[half, g][0],
+                        rhs_scale=moving[half, g][1],
+                        start=len(done) == 1,
+                        stop=len(done) == PASSES,
                     )
                 if len(done) == PASSES:
-                    closed.append(tile)
-                    closed_at[tile] = issued[0]
                     opened.remove(tile)
+                    closed.append(tile)
             return budget
 
-        def drain(lag):
-            tails = []
-            for mt, half in [t for t in closed if issued[0] - closed_at[t] >= lag]:
-                acc, bank, done = state[mt, half]
-                cols = slice(half * N_TILE, (half + 1) * N_TILE)
-                pre = work.tile([P, N_TILE], F32, name="pre", bufs=6)
-                nc.vector.tensor_tensor(out=pre[:], in0=acc[:], in1=bias_row[:, cols], op=ADD)
-                free_banks.append(bank)
-                closed.remove((mt, half))
-                tails.append((mt, cols, pre))
-            return tails
+        def add_bias(tile, lo, hi):
+            row, half = tile
+            cols = slice(half * N_TILE + lo, half * N_TILE + hi)
+            pre = work.tile([P, hi - lo], F32, name="pre", bufs=4)
+            nc.vector.tensor_tensor(out=pre[:], in0=state[tile][0][:, lo:hi], in1=bias_values[:, cols], op=ADD)
+            return row, cols, pre
 
-        def tick(n):
-            issued[0] = issued[0] + n
+        def empty_banks(tiles):
+            sums = []
+            for tile in [t for t in tiles if t in closed]:
+                sums.append(add_bias(tile, 0, N_TILE))
+                closed.remove(tile)
+                free_banks.append(state[tile][1])
+            return sums
 
-        def warm_up(n):
-            codes, scales = rhs[0, 0]
-            for k in range(n):
-                spare = psum.tile([P, N_TILE], F32, name="spare", tag="acc%d" % (ACC_BANKS - 1))
-                nc.tensor.matmul_mx(out=spare[:], lhsT=codes[:, 0:P], lhsT_scale=scales[:, 0:P], rhs=codes, rhs_scale=scales, start=True, stop=True)
-
-        def finish(tails):
-            for mt, cols, pre in tails:
-                y = work.tile([P, N_TILE], F32, name="y", bufs=4)
+        def finish(sums):
+            for row, cols, pre in sums:
+                y = work.tile([P, cols.stop - cols.start], F32, name="y", bufs=4)
                 nc.scalar.activation(out=y[:], in_=pre[:], func=TANH)
-                nc.sync.dma_start(out=out_rows[:, mt, cols], in_=y[:])
+                nc.sync.dma_start(out=out_rows[:, row, cols], in_=y[:])
 
-        def spread_bias():
-            bias_words = bias_sb[:].bitcast(F32)
-            bias_ps = psum.tile([P, 4, P], F32, name="bias_ps", tag="acc3")
-            for s in range(4):
-                nc.tensor.transpose(bias_ps[:, s, :], bias_words[:, s:s + 1].to_broadcast([P, P]), ident[:])
-            nc.scalar.copy(out=bias_all[:], in_=bias_ps[:].rearrange("p s q -> p q s"))
-
-        def pieces_of(rnd, engine):
-            first = 1 + sum(len(r) for r in ROUND_PIECES[:rnd])
-            if rnd >= len(ROUND_PIECES):
-                return []
-            return [first + n for n, e in enumerate(ROUND_PIECES[rnd]) if e == engine]
-
-        interleave(0, "vector", tag="stage0")
+        new_grouped(0, "shared0", 1)
+        group_columns(0, nc.vector.tensor_copy, 0, N_TILE)
         quantize_piece(0)
-        warm_up(0)
-        multiply_z(0, 0)
-        for p in pieces_of(0, "scalar")[:1]:
-            interleave(p, "scalar", 0, 256)
-        for mt in range(M_TILES):
-            for p in pieces_of(mt, "gpsimd"):
-                interleave(p, "gpsimd", 0, G_COLS, tag="stage%d" % (mt % 2))
-            for p in pieces_of(mt, "scalar")[:1]:
-                interleave(p, "scalar", 256, N_TILE)
-            if G_COLS < N_TILE:
-                for p in pieces_of(mt, "gpsimd"):
-                    interleave(p, "scalar", G_COLS, N_TILE)
-            multiply_z(mt, 1)
-            turn_tile(mt)
-            if mt == 0:
-                spread_bias()
-            if mt + 1 < M_TILES:
-                multiply_z(mt + 1, 0)
-            if mt <= -1:
-                warm_up(0)
-            tails = drain(0)
-            left = multiply(11)
-            finish(tails)
-            for p in pieces_of(mt, "scalar")[1:]:
-                interleave(p, "scalar")
-            for p in pieces_of(mt + 1, "scalar")[:1]:
-                interleave(p, "scalar", 0, 256)
-            pass
-            for p in pieces_of(mt, "vector"):
-                interleave(p, "vector")
-            for p in pieces_of(mt, "scalar") + pieces_of(mt, "gpsimd") + pieces_of(mt, "vector"):
-                quantize_piece(p)
-                left = multiply(left)
-            quantize_tile(mt)
-            left = multiply(left)
-            if mt <= -1:
-                warm_up(min(left, 0))
-        while waiting or opened or len(closed) > 1:
-            multiply(PASSES)
-            if waiting or opened:
-                finish(drain(1))
-            else:
-                finish(drain(1))
-        mt, half = closed[0]
-        acc = state[mt, half][0]
-        tails = []
-        for part in range(2):
-            cols = slice(half * N_TILE + part * 256, half * N_TILE + (part + 1) * 256)
-            pre = work.tile([P, 256], F32, name="pre_last")
-            nc.vector.tensor_tensor(out=pre[:], in0=acc[:, part * 256:(part + 1) * 256], in1=bias_row[:, cols], op=ADD)
-            y = work.tile([P, 256], F32, name="y_last")
-            nc.scalar.activation(out=y[:], in_=pre[:], func=TANH)
-            nc.sync.dma_start(out=out_rows[:, mt, cols], in_=y[:])
+        form_z(0, 0)
+        group_on_scalar(1)
+        group_on_gpsimd(2, "shared0", 512)
+        new_grouped(3, "scalar_piece", 2)
+        group_columns(3, nc.scalar.copy, 0, 384)
+        form_z(0, 1)
+        turn_row_tile(0)
+        turn_b_out(1)
+        spread_bias()
+        form_z(1, 0)
+        group_columns(3, nc.vector.tensor_copy, 384, N_TILE)
+        quantize_piece(1)
+        quantize_row_tile(0)
+        multiply(ROUND_PASSES, 0)
+        group_on_scalar(4)
+        for piece in (3, 2):
+            quantize_piece(piece)
+            multiply(ROUND_PASSES, 0)
+        closed_before_tile = []
+        for row in range(1, ROW_TILES):
+            pieces = round_pieces(row)
+            for piece in pieces[1:]:
+                group_on_gpsimd(piece, "shared%d" % ((row + 1) % 2), GPSIMD_COLS)
+            form_z(row, 1)
+            sums = empty_banks(closed_before_tile)
+            closed_before_turn = list(closed)
+            turn_row_tile(row)
+            finish(sums)
+            if row == 9:
+                turn_b_out(1)
+            if row + 1 < ROW_TILES:
+                form_z(row + 1, 0)
+            if row == 1:
+                turn_b_back(1)
+            budget = multiply(ROUND_PASSES, 1)
+            for piece in round_pieces(row + 1)[:1]:
+                group_on_scalar(piece)
+            for piece in pieces:
+                quantize_piece(piece)
+                budget = multiply(budget, 1)
+            sums = empty_banks(closed_before_turn)
+            budget = multiply(budget, 1)
+            finish(sums)
+            closed_before_tile = list(closed)
+            quantize_row_tile(row)
+            sums = empty_banks([] if free_banks else closed_before_tile[:1])
+            multiply(budget, 0)
+            finish(sums)
+        while waiting or opened:
+            multiply(PASSES, 0)
+            finish(empty_banks(closed[:-1]))
+        finish(empty_banks(closed[:-1]))
+        last = closed[0]
+        for lo in range(0, N_TILE, N_TILE // 2):
+            finish([add_bias(last, lo, lo + N_TILE // 2)])

@@ -25,21 +25,25 @@ HALVES = N // N_TILE
 Z_PASSES = I * J // K_PASS
 X_PASSES = D // K_PASS
 PASSES = Z_PASSES + X_PASSES
-I_PER_PASS = K_PASS // J
-J_PAIRS = J // PACK
-B_GROUP = P // J_PAIRS
 PIECES = HALVES * PASSES
-ACC_BANKS = 4
+BANK_PASSES = 2
+Z_PARTS = Z_PASSES // BANK_PASSES
+I_PER_PASS = K_PASS // J
+J_DUOS = J // PACK
+B_GROUP = P // J_DUOS
+SPREAD = 4
+RUN = 4
+
 TURN_BANKS = 3
+ACC_BANKS = 4
+
 GPSIMD_COLS = 416
-ROUND_PASSES = 13
-MAX_EARLY = 3
+SCALAR_COLS_PIECE_3 = 320
+HELD_BACK = 2
 
 
 def round_pieces(row):
-    if row == 0:
-        return [1, 2, 3]
-    return [p for p in (2 * row + 2, 2 * row + 3) if p < PIECES]
+    return [piece for piece in (2 * row + 2, 2 * row + 3) if piece < PIECES]
 
 
 def tile_tensor_product_core_s2_kernel(tc, a, b, c, core, x, w, bias, out):
@@ -81,13 +85,15 @@ def tile_tensor_product_core_s2_kernel(tc, a, b, c, core, x, w, bias, out):
         nc.sync.dma_start(out=c_sb[:], in_=c.rearrange("i (r s) -> (i r) s", s=I * J // P))
         load_piece(0)
         nc.sync.dma_start(out=a_sb[:], in_=a.rearrange("(p r) i -> p (r i)", r=ROW_TILES))
-        for row in range(ROW_TILES):
+        for piece in (1, 2, 3):
+            load_piece(piece)
+        load_x(0)
+        load_b(1)
+        nc.sync.dma_start(out=bias_sb[:], in_=bias.rearrange("(p s) -> p s", p=P))
+        for row in range(1, ROW_TILES):
             for piece in round_pieces(row):
                 load_piece(piece)
             load_x(row)
-            if row == 0:
-                load_b(1)
-                nc.sync.dma_start(out=bias_sb[:], in_=bias.rearrange("(p s) -> p s", p=P))
 
         ident = keep.tile([P, P], F32, name="ident")
         make_identity(nc, ident[:])
@@ -98,10 +104,10 @@ def tile_tensor_product_core_s2_kernel(tc, a, b, c, core, x, w, bias, out):
         b_turned = {}
 
         def turn_b_out(group):
-            pairs = b_sb[group][:].bitcast(F32)
+            duos = b_sb[group][:].bitcast(F32)
             ps = psum.tile([P, 2, P], F32, name="b_turn", tag="turn", bufs=TURN_BANKS)
             for u in range(2):
-                nc.tensor.transpose(ps[:, u, :], pairs[:, u::2], ident[:])
+                nc.tensor.transpose(ps[:, u, :], duos[:, u::2], ident[:])
             b_turned[group] = work.tile([P, 2, P], F32, name="b_turned")
             nc.scalar.copy(out=b_turned[group][:], in_=ps[:])
 
@@ -109,42 +115,43 @@ def tile_tensor_product_core_s2_kernel(tc, a, b, c, core, x, w, bias, out):
             for u in range(2):
                 nc.tensor.transpose(b_ps[:, group, u, :], b_turned[group][:, u, :], ident[:])
 
+        def spread(columns):
+            ps = psum.tile([P, SPREAD, P], F32, name="spread", tag="turn", bufs=TURN_BANKS)
+            for s, column in enumerate(columns):
+                nc.tensor.transpose(ps[:, s, :], column.to_broadcast([P, P]), ident[:])
+            return ps
+
         turn_b_out(0)
-        c_words = c_sb[:].bitcast(F32)
-        c_all = keep.tile([P, I, 2, J_PAIRS], F32, name="c_all")
+        c_duos = c_sb[:].bitcast(F32)
+        c_all = keep.tile([P, I, 2, J_DUOS], F32, name="c_all")
         for u in range(2):
-            ps = psum.tile([P, 4, P], F32, name="c_spread", tag="turn", bufs=TURN_BANKS)
-            for s in range(4):
-                word = 2 * s + u
-                nc.tensor.transpose(ps[:, s, :], c_words[:, word:word + 1].to_broadcast([P, P]), ident[:])
+            ps = spread([c_duos[:, 2 * s + u:2 * s + u + 1] for s in range(SPREAD)])
             nc.scalar.copy(
-                out=c_all[:, :, u, :].rearrange("p i (r s) -> p i r s", s=4),
+                out=c_all[:, :, u, :].rearrange("p i (r s) -> p i r s", s=SPREAD),
                 in_=ps[:].rearrange("p s (i r) -> p i r s", i=I),
             )
         turn_b_back(0)
         b_values = b_ps[:].rearrange("p h u q -> p (h u q)").bitcast(BF16)
-        b_values = b_values.rearrange("p (h u r e) -> p h u r e", u=2, r=B_GROUP, e=2 * J_PAIRS)
+        b_values = b_values.rearrange("p (h u r e) -> p h u r e", u=2, r=B_GROUP, e=2 * J_DUOS)
         c_values = c_all[:].rearrange("p i u q -> p (i u q)").bitcast(BF16)
         c_values = c_values.rearrange("p (i u e) -> p i u e", i=I, u=2)
 
-        bias_all = keep.tile([P, P, 4], F32, name="bias_all")
+        bias_all = keep.tile([P, P, SPREAD], F32, name="bias_all")
         bias_values = bias_all[:].rearrange("p q s -> p (q s)").bitcast(BF16)
 
         def spread_bias():
-            words = bias_sb[:].bitcast(F32)
-            ps = psum.tile([P, 4, P], F32, name="bias_spread", tag="turn", bufs=TURN_BANKS)
-            for s in range(4):
-                nc.tensor.transpose(ps[:, s, :], words[:, s:s + 1].to_broadcast([P, P]), ident[:])
+            duos = bias_sb[:].bitcast(F32)
+            ps = spread([duos[:, s:s + 1] for s in range(SPREAD)])
             nc.scalar.copy(out=bias_all[:], in_=ps[:].rearrange("p s q -> p q s"))
 
-        z_sb, z_turned, x_turned, grouped, stationary, moving = {}, {}, {}, {}, {}, {}
+        z_sb, z_turned, x_sorted, x_turned, stationary = {}, {}, {}, {}, {}
 
         def form_z(row, part):
-            z = work.tile([P, 2, 2, I_PER_PASS, 2 * J_PAIRS], BF16, name="z", bufs=3)
+            z = work.tile([P, BANK_PASSES, 2, I_PER_PASS, 2 * J_DUOS], BF16, name="z", bufs=3)
             z_sb[row, part] = z
-            for g in range(2):
+            for g in range(BANK_PASSES):
                 for il in range(I_PER_PASS):
-                    i = (2 * part + g) * I_PER_PASS + il
+                    i = (BANK_PASSES * part + g) * I_PER_PASS + il
                     nc.vector.scalar_tensor_tensor(
                         out=z[:, g, :, il, :],
                         in0=b_values[:, row // B_GROUP, :, row % B_GROUP, :],
@@ -154,20 +161,30 @@ def tile_tensor_product_core_s2_kernel(tc, a, b, c, core, x, w, bias, out):
                         op1=MULT,
                     )
 
+        def sort_x(row):
+            x_sorted[row] = work.tile([P, X_PASSES, 2, P], F32, name="x_sorted")
+            duos = x_sb[row][:].bitcast(F32)
+            nc.scalar.copy(out=x_sorted[row][:], in_=duos.rearrange("m (g p u) -> m g u p", g=X_PASSES, u=2))
+
         def turn(sources, dst):
-            ps = psum.tile([P, 2, 2, P], F32, name="turn", tag="turn", bufs=TURN_BANKS)
+            ps = psum.tile([P, BANK_PASSES, 2, P], F32, name="turn", tag="turn", bufs=TURN_BANKS)
             for n, source in enumerate(sources):
                 nc.tensor.transpose(ps[:, n // 2, n % 2, :], source, ident[:])
             nc.scalar.copy(out=dst, in_=ps[:].rearrange("p g u m -> p g m u"))
 
-        def turn_row_tile(row):
+        def turn_row_tile(row, x_tag):
             z_turned[row] = work.tile([P, Z_PASSES, P, 2], F32, name="z_turned", align_bytes=64)
-            for part in range(2):
-                pairs = z_sb[row, part][:].rearrange("p g u i e -> p (g u i e)").bitcast(F32)
-                turn([pairs[:, P * n:P * (n + 1)] for n in range(4)], z_turned[row][:, 2 * part:2 * part + 2, :, :])
-            x_turned[row] = work.tile([P, X_PASSES, P, 2], F32, name="x_turned", tag=("shared%d" % (row % 2)) if row else "x0", bufs=1, align_bytes=64)
-            pairs = x_sb[row][:].bitcast(F32)
-            turn([pairs[:, 2 * P * g + u:2 * P * (g + 1):2] for g in range(2) for u in range(2)], x_turned[row][:])
+            for part in range(Z_PARTS):
+                duos = z_sb[row, part][:].rearrange("m g u i e -> m (g u i e)").bitcast(F32)
+                passes = slice(BANK_PASSES * part, BANK_PASSES * (part + 1))
+                turn([duos[:, P * n:P * (n + 1)] for n in range(SPREAD)], z_turned[row][:, passes, :, :])
+            x_turned[row] = work.tile([P, X_PASSES, P, 2], F32, name="x_turned", tag=x_tag, bufs=1, align_bytes=64)
+            if row in x_sorted:
+                sources = [x_sorted[row][:, g, u, :] for g in range(X_PASSES) for u in range(2)]
+            else:
+                duos = x_sb[row][:].bitcast(F32)
+                sources = [duos[:, 2 * P * g + u:2 * P * (g + 1):2] for g in range(X_PASSES) for u in range(2)]
+            turn(sources, x_turned[row][:])
 
         def quantize(values, width, fmt, name):
             codes = keep.tile([P, width], U32, name=name + "_codes", align_bytes=64)
@@ -186,17 +203,18 @@ def tile_tensor_product_core_s2_kernel(tc, a, b, c, core, x, w, bias, out):
                     cols = slice(g * P, (g + 1) * P)
                     stationary[row, first + g] = (codes[:, cols].bitcast(fmt), scales[:, cols])
 
+        grouped, moving = {}, {}
+
         def new_grouped(piece, tag, bufs):
             grouped[piece] = work.tile([P, N_TILE, PACK], BF16, name="grouped", tag=tag, bufs=bufs, align_bytes=64)
 
         def group_columns(piece, copy, lo, hi):
             copy(
-                out=grouped[piece][:, lo:hi, :].rearrange("p (q e) t -> p q t e", e=4),
-                in_=raw[piece][:, :, lo:hi].rearrange("p t (q e) -> p q t e", e=4),
+                out=grouped[piece][:, lo:hi, :].rearrange("p (q e) t -> p q t e", e=RUN),
+                in_=raw[piece][:, :, lo:hi].rearrange("p t (q e) -> p q t e", e=RUN),
             )
 
-        def group_on_gpsimd(piece, tag, cols):
-            new_grouped(piece, tag, 1)
+        def group_columns_on_gpsimd(piece, cols):
             nc.gpsimd.tensor_scalar(
                 out=grouped[piece][:, 0:cols, :],
                 in0=raw[piece][:, :, 0:cols].rearrange("p t n -> p n t"),
@@ -205,8 +223,6 @@ def tile_tensor_product_core_s2_kernel(tc, a, b, c, core, x, w, bias, out):
                 op0=MULT,
                 op1=ADD,
             )
-            if cols < N_TILE:
-                group_columns(piece, nc.scalar.copy, cols, N_TILE)
 
         def group_on_scalar(piece):
             new_grouped(piece, "scalar_piece", 2)
@@ -214,16 +230,13 @@ def tile_tensor_product_core_s2_kernel(tc, a, b, c, core, x, w, bias, out):
 
         def quantize_piece(piece):
             values = grouped[piece][:].rearrange("p n t -> p (n t)")
-            codes, scales = quantize(values, N_TILE, E4M3, "w%d" % piece)
+            codes, scales = quantize(values, N_TILE, E4M3, "piece%d" % piece)
             moving[divmod(piece, PASSES)] = (codes[:].bitcast(E4M3), scales[:])
 
         waiting = [(row, half) for half in range(HALVES) for row in range(ROW_TILES)]
         opened, closed = [], []
         free_banks = list(range(ACC_BANKS))
         state = {}
-
-        def lacks_pieces(tile):
-            return any((tile[1], g) not in moving for g in range(PASSES))
 
         def multiply(budget, reserve):
             for tile in opened + waiting:
@@ -232,9 +245,8 @@ def tile_tensor_product_core_s2_kernel(tc, a, b, c, core, x, w, bias, out):
                 if tile not in state:
                     if not ready or budget == 0 or not free_banks:
                         continue
-                    if half > 0 and lacks_pieces(tile):
-                        if len([t for t in opened if lacks_pieces(t)]) >= MAX_EARLY or len(free_banks) <= reserve:
-                            continue
+                    if half > 0 and len(ready) < PASSES and len(free_banks) + len(closed) <= reserve:
+                        continue
                     bank = free_banks[0]
                     free_banks.remove(bank)
                     acc = psum.tile([P, N_TILE], F32, name="acc", tag="acc%d" % bank)
@@ -262,7 +274,7 @@ def tile_tensor_product_core_s2_kernel(tc, a, b, c, core, x, w, bias, out):
         def add_bias(tile, lo, hi):
             row, half = tile
             cols = slice(half * N_TILE + lo, half * N_TILE + hi)
-            pre = work.tile([P, hi - lo], F32, name="pre", bufs=4)
+            pre = work.tile([P, hi - lo], F32, name="pre", bufs=ACC_BANKS)
             nc.vector.tensor_tensor(out=pre[:], in0=state[tile][0][:, lo:hi], in1=bias_values[:, cols], op=ADD)
             return row, cols, pre
 
@@ -276,7 +288,7 @@ def tile_tensor_product_core_s2_kernel(tc, a, b, c, core, x, w, bias, out):
 
         def finish(sums):
             for row, cols, pre in sums:
-                y = work.tile([P, cols.stop - cols.start], F32, name="y", bufs=4)
+                y = work.tile([P, cols.stop - cols.start], F32, name="y", bufs=ACC_BANKS)
                 nc.scalar.activation(out=y[:], in_=pre[:], func=TANH)
                 nc.sync.dma_start(out=out_rows[:, row, cols], in_=y[:])
 
@@ -285,56 +297,61 @@ def tile_tensor_product_core_s2_kernel(tc, a, b, c, core, x, w, bias, out):
         quantize_piece(0)
         form_z(0, 0)
         group_on_scalar(1)
-        group_on_gpsimd(2, "shared0", 512)
+        new_grouped(2, "shared0", 1)
+        group_columns_on_gpsimd(2, N_TILE)
         new_grouped(3, "scalar_piece", 2)
-        group_columns(3, nc.scalar.copy, 0, 384)
+        group_columns(3, nc.scalar.copy, 0, SCALAR_COLS_PIECE_3)
         form_z(0, 1)
-        turn_row_tile(0)
+        turn_row_tile(0, "x_turned0")
         turn_b_out(1)
         spread_bias()
         form_z(1, 0)
-        group_columns(3, nc.vector.tensor_copy, 384, N_TILE)
+        group_columns(3, nc.vector.tensor_copy, SCALAR_COLS_PIECE_3, N_TILE)
         quantize_piece(1)
         quantize_row_tile(0)
-        multiply(ROUND_PASSES, 0)
-        group_on_scalar(4)
+        multiply(PASSES, 0)
+        group_on_scalar(round_pieces(1)[0])
         for piece in (3, 2):
             quantize_piece(piece)
-            multiply(ROUND_PASSES, 0)
-        closed_before_tile = []
+            multiply(PASSES, 0)
+
+        closed_before_row_tile = []
         for row in range(1, ROW_TILES):
             pieces = round_pieces(row)
             for piece in pieces[1:]:
-                group_on_gpsimd(piece, "shared%d" % ((row + 1) % 2), GPSIMD_COLS)
+                new_grouped(piece, "shared%d" % ((row + 1) % 2), 1)
+                group_columns_on_gpsimd(piece, GPSIMD_COLS)
+                group_columns(piece, nc.scalar.copy, GPSIMD_COLS, N_TILE)
             form_z(row, 1)
-            sums = empty_banks(closed_before_tile)
+            sums = empty_banks(closed_before_row_tile)
             closed_before_turn = list(closed)
-            turn_row_tile(row)
+            turn_row_tile(row, "shared%d" % (row % 2))
             finish(sums)
-            if row == 9:
-                turn_b_out(1)
             if row + 1 < ROW_TILES:
                 form_z(row + 1, 0)
             if row == 1:
                 turn_b_back(1)
-            budget = multiply(ROUND_PASSES, 1)
-            for piece in round_pieces(row + 1)[:1]:
-                group_on_scalar(piece)
+            budget = multiply(ACC_BANKS * PASSES if pieces else HALVES * PASSES, 1)
+            if round_pieces(row + 1):
+                group_on_scalar(round_pieces(row + 1)[0])
+            elif row + 1 < ROW_TILES:
+                sort_x(row + 1)
             for piece in pieces:
                 quantize_piece(piece)
                 budget = multiply(budget, 1)
             sums = empty_banks(closed_before_turn)
             budget = multiply(budget, 1)
             finish(sums)
-            closed_before_tile = list(closed)
+            closed_before_row_tile = list(closed)
             quantize_row_tile(row)
-            sums = empty_banks([] if free_banks else closed_before_tile[:1])
+            sums = empty_banks([] if free_banks else closed_before_row_tile[:1])
+            if (1, 0) not in moving:
+                budget = min(budget, PASSES - HELD_BACK)
             multiply(budget, 0)
             finish(sums)
+
         while waiting or opened:
             multiply(PASSES, 0)
             finish(empty_banks(closed[:-1]))
-        finish(empty_banks(closed[:-1]))
-        last = closed[0]
-        for lo in range(0, N_TILE, N_TILE // 2):
-            finish([add_bias(last, lo, lo + N_TILE // 2)])
+        for lo in (0, N_TILE // 2):
+            finish([add_bias(closed[0], lo, lo + N_TILE // 2)])

from contextlib import ExitStack

import concourse.mybir as mybir
from concourse.masks import make_identity

M, I, J, D, N = 1024, 16, 128, 1024, 1024
FLOPS = 2 * M * N * (I * J + D)

F32 = mybir.dt.float32
BF16 = mybir.dt.bfloat16
U32 = mybir.dt.uint32
U8 = mybir.dt.uint8
E4M3 = mybir.dt.float8_e4m3fn_x4
E5M2 = mybir.dt.float8_e5m2_x4
MULT = mybir.AluOpType.mult
ADD = mybir.AluOpType.add
TANH = mybir.ActivationFunctionType.Tanh

P = 128
PACK = 4
K_PASS = P * PACK
N_TILE = 512
ROW_TILES = M // P
HALVES = N // N_TILE
Z_PASSES = I * J // K_PASS
X_PASSES = D // K_PASS
PASSES = Z_PASSES + X_PASSES
PIECES = HALVES * PASSES
BANK_PASSES = 2
Z_PARTS = Z_PASSES // BANK_PASSES
I_PER_PASS = K_PASS // J
J_DUOS = J // PACK
B_GROUP = P // J_DUOS
SPREAD = 4
RUN = 4

TURN_BANKS = 3
ACC_BANKS = 4

GPSIMD_COLS = 416
SCALAR_COLS_PIECE_3 = 320
HELD_BACK = 2


def round_pieces(row):
    return [piece for piece in (2 * row + 2, 2 * row + 3) if piece < PIECES]


def tile_tensor_product_core_s2_kernel(tc, a, b, c, core, x, w, bias, out):
    nc = tc.nc
    with ExitStack() as ctx:
        keep = ctx.enter_context(tc.tile_pool(name="keep", bufs=1))
        work = ctx.enter_context(tc.tile_pool(name="work", bufs=2))
        psum = ctx.enter_context(tc.psum_pool(name="psum", bufs=1))
        ctx.enter_context(tc.manual_schedule())

        b_rows = b.rearrange("(p r) j -> p (r j)", r=ROW_TILES)
        x_rows = x.rearrange("(p r) d -> p r d", r=ROW_TILES)
        out_rows = out.rearrange("(p r) n -> p r n", r=ROW_TILES)

        b_sb, x_sb, raw = [], [], []

        def load_b(group):
            tile = keep.tile([P, B_GROUP * J], BF16, name="b_sb%d" % group)
            nc.sync.dma_start(out=tile[:], in_=b_rows[:, group * B_GROUP * J:(group + 1) * B_GROUP * J])
            b_sb.append(tile)

        def load_x(row):
            tile = keep.tile([P, D], BF16, name="x_sb%d" % row)
            nc.sync.dma_start(out=tile[:], in_=x_rows[:, row, :])
            x_sb.append(tile)

        def load_piece(piece):
            half, g = divmod(piece, PASSES)
            source, first = (core, g * K_PASS) if g < Z_PASSES else (w, (g - Z_PASSES) * K_PASS)
            rows = source[first:first + K_PASS, half * N_TILE:(half + 1) * N_TILE]
            tile = keep.tile([P, PACK, N_TILE], BF16, name="raw%d" % piece)
            nc.sync.dma_start(out=tile[:], in_=rows.rearrange("(p t) n -> p t n", t=PACK))
            raw.append(tile)

        c_sb = keep.tile([P, I * J // P], BF16, name="c_sb")
        a_sb = keep.tile([P, ROW_TILES * I], BF16, name="a_sb")
        bias_sb = keep.tile([P, N // P], BF16, name="bias_sb")
        load_b(0)
        nc.sync.dma_start(out=c_sb[:], in_=c.rearrange("i (r s) -> (i r) s", s=I * J // P))
        load_piece(0)
        nc.sync.dma_start(out=a_sb[:], in_=a.rearrange("(p r) i -> p (r i)", r=ROW_TILES))
        for piece in (1, 2, 3):
            load_piece(piece)
        load_x(0)
        load_b(1)
        nc.sync.dma_start(out=bias_sb[:], in_=bias.rearrange("(p s) -> p s", p=P))
        for row in range(1, ROW_TILES):
            for piece in round_pieces(row):
                load_piece(piece)
            load_x(row)

        ident = keep.tile([P, P], F32, name="ident")
        make_identity(nc, ident[:])
        table_warm = keep.tile([P, 1], F32, name="table_warm")
        nc.scalar.activation(out=table_warm[:], in_=ident[:, 0:1], func=TANH)

        b_ps = psum.tile([P, ROW_TILES // B_GROUP, 2, P], F32, name="b_ps")
        b_turned = {}

        def turn_b_out(group):
            duos = b_sb[group][:].bitcast(F32)
            ps = psum.tile([P, 2, P], F32, name="b_turn", tag="turn", bufs=TURN_BANKS)
            for u in range(2):
                nc.tensor.transpose(ps[:, u, :], duos[:, u::2], ident[:])
            b_turned[group] = work.tile([P, 2, P], F32, name="b_turned")
            nc.scalar.copy(out=b_turned[group][:], in_=ps[:])

        def turn_b_back(group):
            for u in range(2):
                nc.tensor.transpose(b_ps[:, group, u, :], b_turned[group][:, u, :], ident[:])

        def spread(columns):
            ps = psum.tile([P, SPREAD, P], F32, name="spread", tag="turn", bufs=TURN_BANKS)
            for s, column in enumerate(columns):
                nc.tensor.transpose(ps[:, s, :], column.to_broadcast([P, P]), ident[:])
            return ps

        turn_b_out(0)
        c_duos = c_sb[:].bitcast(F32)
        c_all = keep.tile([P, I, 2, J_DUOS], F32, name="c_all")
        for u in range(2):
            ps = spread([c_duos[:, 2 * s + u:2 * s + u + 1] for s in range(SPREAD)])
            nc.scalar.copy(
                out=c_all[:, :, u, :].rearrange("p i (r s) -> p i r s", s=SPREAD),
                in_=ps[:].rearrange("p s (i r) -> p i r s", i=I),
            )
        turn_b_back(0)
        b_values = b_ps[:].rearrange("p h u q -> p (h u q)").bitcast(BF16)
        b_values = b_values.rearrange("p (h u r e) -> p h u r e", u=2, r=B_GROUP, e=2 * J_DUOS)
        c_values = c_all[:].rearrange("p i u q -> p (i u q)").bitcast(BF16)
        c_values = c_values.rearrange("p (i u e) -> p i u e", i=I, u=2)

        bias_all = keep.tile([P, P, SPREAD], F32, name="bias_all")
        bias_values = bias_all[:].rearrange("p q s -> p (q s)").bitcast(BF16)

        def spread_bias():
            duos = bias_sb[:].bitcast(F32)
            ps = spread([duos[:, s:s + 1] for s in range(SPREAD)])
            nc.scalar.copy(out=bias_all[:], in_=ps[:].rearrange("p s q -> p q s"))

        z_sb, z_turned, x_sorted, x_turned, stationary = {}, {}, {}, {}, {}

        def form_z(row, part):
            z = work.tile([P, BANK_PASSES, 2, I_PER_PASS, 2 * J_DUOS], BF16, name="z", bufs=3)
            z_sb[row, part] = z
            for g in range(BANK_PASSES):
                for il in range(I_PER_PASS):
                    i = (BANK_PASSES * part + g) * I_PER_PASS + il
                    nc.vector.scalar_tensor_tensor(
                        out=z[:, g, :, il, :],
                        in0=b_values[:, row // B_GROUP, :, row % B_GROUP, :],
                        scalar=a_sb[:, row * I + i:row * I + i + 1],
                        in1=c_values[:, i, :, :],
                        op0=MULT,
                        op1=MULT,
                    )

        def sort_x(row):
            x_sorted[row] = work.tile([P, X_PASSES, 2, P], F32, name="x_sorted")
            duos = x_sb[row][:].bitcast(F32)
            nc.scalar.copy(out=x_sorted[row][:], in_=duos.rearrange("m (g p u) -> m g u p", g=X_PASSES, u=2))

        def turn(sources, dst):
            ps = psum.tile([P, BANK_PASSES, 2, P], F32, name="turn", tag="turn", bufs=TURN_BANKS)
            for n, source in enumerate(sources):
                nc.tensor.transpose(ps[:, n // 2, n % 2, :], source, ident[:])
            nc.scalar.copy(out=dst, in_=ps[:].rearrange("p g u m -> p g m u"))

        def turn_row_tile(row, x_tag):
            z_turned[row] = work.tile([P, Z_PASSES, P, 2], F32, name="z_turned", align_bytes=64)
            for part in range(Z_PARTS):
                duos = z_sb[row, part][:].rearrange("m g u i e -> m (g u i e)").bitcast(F32)
                passes = slice(BANK_PASSES * part, BANK_PASSES * (part + 1))
                turn([duos[:, P * n:P * (n + 1)] for n in range(SPREAD)], z_turned[row][:, passes, :, :])
            x_turned[row] = work.tile([P, X_PASSES, P, 2], F32, name="x_turned", tag=x_tag, bufs=1, align_bytes=64)
            if row in x_sorted:
                sources = [x_sorted[row][:, g, u, :] for g in range(X_PASSES) for u in range(2)]
            else:
                duos = x_sb[row][:].bitcast(F32)
                sources = [duos[:, 2 * P * g + u:2 * P * (g + 1):2] for g in range(X_PASSES) for u in range(2)]
            turn(sources, x_turned[row][:])

        def quantize(values, width, fmt, name):
            codes = keep.tile([P, width], U32, name=name + "_codes", align_bytes=64)
            scales = keep.tile([P, width], U8, name=name + "_scales", align_bytes=64)
            nc.vector.quantize_mx(out=codes[:].bitcast(fmt), scales=scales[:], in_=values)
            return codes, scales

        def quantize_row_tile(row):
            for turned, first, passes, fmt, name in (
                (z_turned[row], 0, Z_PASSES, E5M2, "z%d" % row),
                (x_turned[row], Z_PASSES, X_PASSES, E4M3, "x%d" % row),
            ):
                values = turned[:].rearrange("p g m u -> p (g m u)").bitcast(BF16)
                codes, scales = quantize(values, passes * P, fmt, name)
                for g in range(passes):
                    cols = slice(g * P, (g + 1) * P)
                    stationary[row, first + g] = (codes[:, cols].bitcast(fmt), scales[:, cols])

        grouped, moving = {}, {}

        def new_grouped(piece, tag, bufs):
            grouped[piece] = work.tile([P, N_TILE, PACK], BF16, name="grouped", tag=tag, bufs=bufs, align_bytes=64)

        def group_columns(piece, copy, lo, hi):
            copy(
                out=grouped[piece][:, lo:hi, :].rearrange("p (q e) t -> p q t e", e=RUN),
                in_=raw[piece][:, :, lo:hi].rearrange("p t (q e) -> p q t e", e=RUN),
            )

        def group_columns_on_gpsimd(piece, cols):
            nc.gpsimd.tensor_scalar(
                out=grouped[piece][:, 0:cols, :],
                in0=raw[piece][:, :, 0:cols].rearrange("p t n -> p n t"),
                scalar1=1.0,
                scalar2=0.0,
                op0=MULT,
                op1=ADD,
            )

        def group_on_scalar(piece):
            new_grouped(piece, "scalar_piece", 2)
            group_columns(piece, nc.scalar.copy, 0, N_TILE)

        def quantize_piece(piece):
            values = grouped[piece][:].rearrange("p n t -> p (n t)")
            codes, scales = quantize(values, N_TILE, E4M3, "piece%d" % piece)
            moving[divmod(piece, PASSES)] = (codes[:].bitcast(E4M3), scales[:])

        waiting = [(row, half) for half in range(HALVES) for row in range(ROW_TILES)]
        opened, closed = [], []
        free_banks = list(range(ACC_BANKS))
        state = {}

        def multiply(budget, reserve):
            for tile in opened + waiting:
                row, half = tile
                ready = [g for g in range(PASSES) if (row, g) in stationary and (half, g) in moving]
                if tile not in state:
                    if not ready or budget == 0 or not free_banks:
                        continue
                    if half > 0 and len(ready) < PASSES and len(free_banks) + len(closed) <= reserve:
                        continue
                    bank = free_banks[0]
                    free_banks.remove(bank)
                    acc = psum.tile([P, N_TILE], F32, name="acc", tag="acc%d" % bank)
                    state[tile] = (acc, bank, [])
                    waiting.remove(tile)
                    opened.append(tile)
                acc, bank, done = state[tile]
                for g in [g for g in ready if g not in done][:budget]:
                    done.append(g)
                    budget = budget - 1
                    nc.tensor.matmul_mx(
                        out=acc[:],
                        lhsT=stationary[row, g][0],
                        lhsT_scale=stationary[row, g][1],
                        rhs=moving[half, g][0],
                        rhs_scale=moving[half, g][1],
                        start=len(done) == 1,
                        stop=len(done) == PASSES,
                    )
                if len(done) == PASSES:
                    opened.remove(tile)
                    closed.append(tile)
            return budget

        def add_bias(tile, lo, hi):
            row, half = tile
            cols = slice(half * N_TILE + lo, half * N_TILE + hi)
            pre = work.tile([P, hi - lo], F32, name="pre", bufs=ACC_BANKS)
            nc.vector.tensor_tensor(out=pre[:], in0=state[tile][0][:, lo:hi], in1=bias_values[:, cols], op=ADD)
            return row, cols, pre

        def empty_banks(tiles):
            sums = []
            for tile in [t for t in tiles if t in closed]:
                sums.append(add_bias(tile, 0, N_TILE))
                closed.remove(tile)
                free_banks.append(state[tile][1])
            return sums

        def finish(sums):
            for row, cols, pre in sums:
                y = work.tile([P, cols.stop - cols.start], F32, name="y", bufs=ACC_BANKS)
                nc.scalar.activation(out=y[:], in_=pre[:], func=TANH)
                nc.sync.dma_start(out=out_rows[:, row, cols], in_=y[:])

        new_grouped(0, "shared0", 1)
        group_columns(0, nc.vector.tensor_copy, 0, N_TILE)
        quantize_piece(0)
        form_z(0, 0)
        group_on_scalar(1)
        new_grouped(2, "shared0", 1)
        group_columns_on_gpsimd(2, N_TILE)
        new_grouped(3, "scalar_piece", 2)
        group_columns(3, nc.scalar.copy, 0, SCALAR_COLS_PIECE_3)
        form_z(0, 1)
        turn_row_tile(0, "x_turned0")
        turn_b_out(1)
        spread_bias()
        form_z(1, 0)
        group_columns(3, nc.vector.tensor_copy, SCALAR_COLS_PIECE_3, N_TILE)
        quantize_piece(1)
        quantize_row_tile(0)
        multiply(PASSES, 0)
        group_on_scalar(round_pieces(1)[0])
        for piece in (3, 2):
            quantize_piece(piece)
            multiply(PASSES, 0)

        closed_before_row_tile = []
        for row in range(1, ROW_TILES):
            pieces = round_pieces(row)
            for piece in pieces[1:]:
                new_grouped(piece, "shared%d" % ((row + 1) % 2), 1)
                group_columns_on_gpsimd(piece, GPSIMD_COLS)
                group_columns(piece, nc.scalar.copy, GPSIMD_COLS, N_TILE)
            form_z(row, 1)
            sums = empty_banks(closed_before_row_tile)
            closed_before_turn = list(closed)
            turn_row_tile(row, "shared%d" % (row % 2))
            finish(sums)
            if row + 1 < ROW_TILES:
                form_z(row + 1, 0)
            if row == 1:
                turn_b_back(1)
            budget = multiply(ACC_BANKS * PASSES if pieces else HALVES * PASSES, 1)
            if round_pieces(row + 1):
                group_on_scalar(round_pieces(row + 1)[0])
            elif row + 1 < ROW_TILES:
                sort_x(row + 1)
            for piece in pieces:
                quantize_piece(piece)
                budget = multiply(budget, 1)
            sums = empty_banks(closed_before_turn)
            budget = multiply(budget, 1)
            finish(sums)
            closed_before_row_tile = list(closed)
            quantize_row_tile(row)
            sums = empty_banks([] if free_banks else closed_before_row_tile[:1])
            if (1, 0) not in moving:
                budget = min(budget, PASSES - HELD_BACK)
            multiply(budget, 0)
            finish(sums)

        while waiting or opened:
            multiply(PASSES, 0)
            finish(empty_banks(closed[:-1]))
        for lo in (0, N_TILE // 2):
            finish([add_bias(closed[0], lo, lo + N_TILE // 2)])
